import numpy as np
import ml_dtypes


def mxq(x, axis, fmt="e4m3"):
    dtype, down = {"e4m3": (ml_dtypes.float8_e4m3fn, 7), "e5m2": (ml_dtypes.float8_e5m2, 14)}[fmt]
    v = np.moveaxis(np.asarray(x, np.float32).astype(ml_dtypes.bfloat16).astype(np.float64), axis, -1)
    blocks = v.reshape(v.shape[:-1] + (-1, 32))
    amax = np.abs(blocks).max(-1, keepdims=True)
    byte = np.maximum(np.where(amax > 0, np.frexp(amax)[1] - 1 + 127, 0) - down, 1)
    scale = np.exp2(byte - 127.0)
    codes = (blocks / scale).astype(np.float32).astype(dtype).astype(np.float64)
    return np.moveaxis((codes * scale).reshape(v.shape), -1, axis)


WIDE = False


def mx_kscale(k):
    if not WIDE:
        return np.ones(k)
    levels = np.array([18, -18])
    if k % 512:
        return np.exp2(np.random.permutation(np.resize(levels, k // 32))).repeat(32)
    a = np.empty((k // 512, 16))
    for p in range(k // 512):
        a[p, :8] = np.random.permutation(np.resize(levels, 8))
        for g in range(8):
            far = levels[np.abs(levels - a[p, g]) >= 10]
            a[p, g + 8] = far[np.random.randint(len(far))]
    return np.exp2(a.ravel()).repeat(32)


def f64(x):
    return np.asarray(x).astype(np.float64)


def striped(idx):
    return np.tile(np.asarray(idx).reshape(-1, 16).T, (8, 1)).astype(np.uint16)


def unstriped(offs):
    return offs[:16].T.reshape(-1).astype(np.int64)

def planes(y):
    n, m = y.shape
    v = y.astype(np.float32).astype(ml_dtypes.bfloat16).astype(np.float64).reshape(n // 32, 32, m)
    top = np.abs(v).max(1)
    byte = np.clip(np.where(top > 0, np.frexp(top)[1] - 1 + 127 - 7, 1), 1, 254)
    codes = (v * np.exp2(127.0 - byte)[:, None, :]).reshape(n, m).astype(np.float32).astype(ml_dtypes.float8_e4m3fn).view(np.uint8)
    words = codes.reshape(n // 512, 128, 4, m).transpose(0, 1, 3, 2)
    return np.ascontiguousarray(words), np.ascontiguousarray(byte.astype(np.uint8).reshape(n // 512, 16, m))


def setup_inputs():
    n = np.random.standard_normal
    uni = np.random.uniform
    idx = np.random.permutation(2048)[:512]
    f_e = mx_kscale(512)
    return {
        "xT": (0.3 + n((512, 2048))).astype(np.float32),
        "W": (n((512, 512)) / np.sqrt(512) * f_e[:, None]).astype(np.float32),
        "dz": (n((512, 512)) / f_e[:, None]).astype(np.float32),
        "gam": np.tile(uni(0.75, 1.3, 512), (128, 1)).astype(np.float32),
        "offs": striped(idx),
    }


def reference(xT, W, dz, gam, offs):
    idx = unstriped(offs)
    xT_i = f64(xT)[:, idx]
    xr = xT_i.T
    dn = mxq(f64(dz), 0, "e5m2").T @ mxq(f64(W), 0, "e4m3")
    h = f64(gam)[:1] * dn
    s1 = (xr).sum(-1, keepdims=True)
    c = xr - s1 / 512.0
    s2 = (np.square(c)).sum(-1, keepdims=True)
    rstd = 1.0 / np.sqrt(s2 / 512.0)
    n = c * rstd
    h1 = (h).sum(-1, keepdims=True)
    h2 = (h * n).sum(-1, keepdims=True)
    dx = rstd * (h - h1 / 512.0 - n * h2 / 512.0)
    dxt = dx.T
    out_0 = np.zeros((512, 2048))
    out_0[:, idx] = dxt
    return (out_0,) + planes(out_0)

@@ -1,0 +1,226 @@
+from contextlib import ExitStack
+
+import concourse.mybir as mybir
+from concourse.masks import make_identity
+
+F32 = mybir.dt.float32
+BF16 = mybir.dt.bfloat16
+I32 = mybir.dt.int32
+U32 = mybir.dt.uint32
+U16 = mybir.dt.uint16
+U8 = mybir.dt.uint8
+E4M3X4 = mybir.dt.float8_e4m3fn_x4
+E5M2X4 = mybir.dt.float8_e5m2_x4
+ALU = mybir.AluOpType
+ACT = mybir.ActivationFunctionType
+
+P = 128
+D = 512
+E = 512
+SLOTS = 512
+TOKENS = 2048
+LANES = 4
+BLOCKS = SLOTS // P
+HALF = SLOTS // 2
+LIST_ROWS = 16
+CHUNKS = (256, 512, 512, 512, 256)
+SCALAR_WEAVES = (4,)
+
+FLOPS = 2 * SLOTS * E * D
+
+
+def tile_attend_gnorm_ln_pl_kernel(tc, xT, W, dz, gam, offs, out_0, out_1, out_2):
+    nc = tc.nc
+    with ExitStack() as ctx:
+        keep = ctx.enter_context(tc.tile_pool(name="keep", bufs=1))
+        psum = ctx.enter_context(tc.psum_pool(name="psum", bufs=1))
+
+        def sb(name, shape, dtype, tag=""):
+            return keep.tile(shape, dtype, name=name, tag=tag or name, align_bytes=64)
+
+        def list_part(first, count):
+            return offsets[:, first // LIST_ROWS : (first + count) // LIST_ROWS]
+
+        w_raw = sb("w_raw", [P, LANES, D], F32)
+        nc.sync.dma_start(out=w_raw[:], in_=W.rearrange("(p j) d -> p j d", j=LANES))
+        dz_rows = dz.rearrange("(p j) i -> p j i", j=LANES)
+        dz_raw = []
+        for a in range(2):
+            raw = sb("dz_raw%d" % a, [P, LANES, HALF], F32)
+            nc.sync.dma_start(out=raw[:], in_=dz_rows[:, :, a * HALF : (a + 1) * HALF])
+            dz_raw.append(raw)
+        offsets = keep.tile([P, SLOTS // LIST_ROWS], U16, name="offsets")
+        nc.sync.dma_start(offsets[:], offs)
+        gam_col = sb("gam_col", [P, LANES], F32)
+        nc.scalar.dma_start(out=gam_col[:], in_=gam[0:1, :].rearrange("o (p t) -> (o p) t", t=LANES))
+        x_planes = xT.rearrange("(p t) c -> t p c", t=LANES)
+        x_win = []
+        for t in range(LANES):
+            win = sb("x_win%d" % t, [P, TOKENS], F32)
+            nc.sync.dma_start(out=win[:], in_=x_planes[t])
+            x_win.append(win)
+
+        ident = sb("ident", [P, P], F32)
+        nc.vector.memset(ident[:], 0.0)
+        make_identity(nc, ident[:], nomemset=True)
+        moments = sb("moments", [P, BLOCKS, LANES + 1, 3], F32)
+        nc.vector.memset(moments[:], float(P))
+        warm = sb("warm", [P, 1], F32)
+        nc.scalar.activation(warm[:], moments[:, 0, 0, 0:1], ACT.Sqrt)
+
+        y_win = []
+        for t in range(LANES):
+            win = sb("y_win%d" % t, [P, TOKENS], F32)
+            nc.vector.memset(win[:].bitcast(I32), 0)
+            y_win.append(win)
+
+        gam_ps = psum.tile([P, LANES, P], F32, name="gam_ps", tag="x_bank3")
+        for t in range(LANES):
+            nc.tensor.transpose(gam_ps[:, t, :], gam_col[:, t : t + 1].to_broadcast([P, P]), ident[:])
+        gam_row = sb("gam_row", [P, D], F32)
+        nc.scalar.copy(gam_row[:], gam_ps[:].rearrange("q t p -> q (t p)"))
+
+        w_bf = sb("w_bf", [P, D * LANES], BF16)
+        w_dst = w_bf[:].rearrange("p (t m j) -> p m t j", t=LANES, j=LANES)
+        w_src = w_raw[:].rearrange("p j (m t) -> p m t j", t=LANES)
+        nc.scalar.copy(w_dst, w_src)
+        w_codes = sb("w_codes", [P, D], U32)
+        w_scales = sb("w_scales", [P, D], U8)
+        dz_bf = [sb("dz_bf%d" % a, [P, HALF, LANES], BF16) for a in range(2)]
+        for a in range(2):
+            nc.vector.tensor_copy(dz_bf[a][:], dz_raw[a][:].rearrange("p j i -> p i j"))
+
+        dn = []
+        for a in range(2):
+            codes = sb("dz_codes%d" % a, [P, HALF], U32)
+            scales = sb("dz_scales%d" % a, [P, HALF], U8)
+            nc.vector.quantize_mx(
+                out=codes[:].bitcast(E5M2X4), scales=scales[:], in_=dz_bf[a][:].rearrange("p i j -> p (i j)"))
+            if a == 0:
+                nc.vector.quantize_mx(out=w_codes[:].bitcast(E4M3X4), scales=w_scales[:], in_=w_bf[:])
+            for b in range(2):
+                acc = psum.tile([P, D], F32, name="dn%d" % (2 * a + b), tag="wide", bufs=4)
+                nc.tensor.matmul_mx(
+                    out=acc[:],
+                    lhsT=codes[:, b * P : (b + 1) * P].bitcast(E5M2X4),
+                    lhsT_scale=scales[:, b * P : (b + 1) * P],
+                    rhs=w_codes[:].bitcast(E4M3X4),
+                    rhs_scale=w_scales[:],
+                    start=True,
+                    stop=True,
+                )
+                dn.append(acc)
+
+        h1 = sb("h1", [P, BLOCKS], F32)
+        h = [sb("h_block%d" % j, [P, D], F32) for j in range(BLOCKS)]
+        unused = sb("unused", [P, BLOCKS, P], F32)
+        turned = [psum.tile([P, D], F32, name="turned%d" % j, tag="x_bank%d" % j) for j in range(BLOCKS)]
+        for t in range(LANES):
+            plane = slice(t * P, (t + 1) * P)
+            gathered = sb("xg%d" % t, [P, SLOTS], F32)
+            parts = [(0, SLOTS)] if t < LANES - 1 else [(0, HALF), (HALF, HALF)]
+            for first, count in parts:
+                nc.vector.tensor_copy(gathered[:, first : first + count], x_win[t][:].indirect(list_part(first, count)))
+            for j in range(BLOCKS):
+                nc.tensor.transpose(turned[j][:, plane], gathered[:, j * P : (j + 1) * P], ident[:])
+            if t < 2:
+                for j in (2 * t, 2 * t + 1):
+                    nc.vector.scalar_tensor_tensor(
+                        h[j][:], dn[j][:], 1.0, gam_row[:], ALU.mult, ALU.mult, accum_out=h1[:, j : j + 1])
+            if t < LANES - 1:
+                for a in range(2):
+                    for j in (2 * a, 2 * a + 1):
+                        nc.scalar.activation(
+                            unused[:, j, :], turned[j][:, plane], ACT.Copy, scale=1.0 / P, accum_out=moments[:, j, t, 1:2])
+                    for j in (2 * a, 2 * a + 1):
+                        nc.scalar.activation(
+                            unused[:, j, :], turned[j][:, plane], ACT.Square,
+                            scale=-1.0, bias=moments[:, j, t, 1:2], accum_out=moments[:, j, t, 2:3])
+        h_mean = sb("h_mean", [P, BLOCKS], F32)
+        neg_h_mean = sb("neg_h_mean", [P, BLOCKS], F32)
+        nc.vector.tensor_scalar(h_mean[:], h1[:], 1.0 / D, None, ALU.mult)
+        nc.vector.tensor_scalar(neg_h_mean[:], h1[:], -1.0 / D, None, ALU.mult)
+
+        products = sb("products", [P, BLOCKS, D], F32)
+        xh = sb("xh", [P, BLOCKS], F32)
+        mv = sb("mv", [P, BLOCKS, 2], F32)
+        inv_var = sb("inv_var", [P, BLOCKS], F32)
+        rstd = sb("rstd", [P, BLOCKS], F32)
+        part = sb("part", [P, BLOCKS], F32)
+        neg_mean = sb("neg_mean", [P, BLOCKS], F32)
+        slope = sb("slope", [P, BLOCKS], F32)
+        shift = sb("shift", [P, BLOCKS], F32)
+        rstd_row = sb("rstd_row", [P, SLOTS], F32)
+        last = LANES - 1
+        u = []
+        backs = [sb("back%d" % t, [P, SLOTS], F32) for t in range(LANES)]
+
+        def turn_back(t, first, count, acc):
+            for j in range(first // P, (first + count) // P):
+                dst = acc[:, j * P - first : (j + 1) * P - first]
+                nc.tensor.matmul(dst, h[j][:, t * P : (t + 1) * P], ident[:], start=True, stop=False, is_transpose=True)
+                nc.tensor.matmul(dst, u[j][:, t * P : (t + 1) * P], ident[:], start=False, stop=True, is_transpose=True)
+            nc.scalar.copy(backs[t][:, first : first + count], acc[:])
+
+        for a in range(2):
+            pair = slice(2 * a, 2 * a + 2)
+            both = (2 * a, 2 * a + 1)
+            for j in both:
+                nc.vector.bn_stats(moments[:, j, last:, :].rearrange("p t s -> p (t s)"), turned[j][:, last * P :])
+            for j in both:
+                nc.vector.bn_aggr(mv[:, j, :], moments[:, j].rearrange("p t s -> p (t s)"))
+            for j in both:
+                col = slice(j, j + 1)
+                nc.vector.scalar_tensor_tensor(
+                    products[:, j, :], turned[j][:], 1.0 / D, h[j][:], ALU.mult, ALU.mult, accum_out=xh[:, col])
+                if j == both[0]:
+                    nc.vector.reciprocal(inv_var[:, pair], mv[:, pair, 1])
+                    nc.vector.tensor_scalar(neg_mean[:, pair], mv[:, pair, 0], -1.0, None, ALU.mult)
+                    nc.vector.tensor_tensor(part[:, pair], mv[:, pair, 0], h_mean[:, pair], ALU.mult)
+                nc.vector.tensor_scalar(slope[:, col], part[:, col], xh[:, col], inv_var[:, col], ALU.subtract, ALU.mult)
+                nc.scalar.activation(shift[:, col], slope[:, col], ACT.Identity, scale=neg_mean[:, col], bias=neg_h_mean[:, col])
+                uj = sb("u%d" % j, [P, D], F32)
+                nc.scalar.activation(uj[:], turned[j][:], ACT.Identity, scale=slope[:, col], bias=shift[:, col])
+                u.append(uj)
+            nc.scalar.activation(rstd[:, pair], inv_var[:, pair], ACT.Sqrt)
+            row_ps = psum.tile([P, HALF], F32, name="row_ps", tag="wide", bufs=4)
+            for b in range(2):
+                j = 2 * a + b
+                nc.tensor.transpose(row_ps[:, b * P : (b + 1) * P], rstd[:, j : j + 1].to_broadcast([P, P]), ident[:])
+            nc.scalar.copy(rstd_row[:, a * HALF : (a + 1) * HALF], row_ps[:])
+            turn_back(0, a * HALF, HALF, psum.tile([P, HALF], F32, name="back_half", tag="wide", bufs=4))
+        for t in range(1, LANES):
+            turn_back(t, 0, SLOTS, psum.tile([P, SLOTS], F32, name="back_whole", tag="x_bank%d" % (t - 1)))
+
+        starts = [sum(CHUNKS[:k]) for k in range(len(CHUNKS))]
+        former = ("u3", "h_block3", "u2", "h_block2", "u1")
+        y_planes = out_0.rearrange("(p t) c -> t p c", t=LANES)
+        pairs = [sb("pairs%d" % k, [P, 2, width, 2], BF16, tag=former[k]) for k, width in enumerate(CHUNKS)]
+        for t in range(LANES):
+            back = backs[t]
+            parts = [(0, HALF), (HALF, HALF)] if t == 0 else [(0, SLOTS)]
+            for first, count in parts:
+                nc.vector.tensor_tensor(
+                    y_win[t][:].indirect(list_part(first, count)), back[:, first : first + count],
+                    rstd_row[:, first : first + count], ALU.mult)
+            nc.sync.dma_start(out=y_planes[t], in_=y_win[t][:])
+            for k, width in enumerate(CHUNKS):
+                nc.scalar.copy(pairs[k][:, t // 2, :, t % 2], y_win[t][:, starts[k] : starts[k] + width])
+
+        words_out = out_1[0].rearrange("p c l -> p (c l)").bitcast(I32)
+        y_scales = sb("y_scales", [P, TOKENS], U8)
+        for k, width in enumerate(CHUNKS):
+            woven = sb("woven%d" % k, [P, width * LANES], BF16)
+            src = pairs[k][:].rearrange("p a c b -> p (a c b)").bitcast(F32).rearrange("p (a c) -> p c a", a=2)
+            dst = woven[:].bitcast(F32).rearrange("p (c a) -> p c a", a=2)
+            if k in SCALAR_WEAVES:
+                nc.scalar.copy(dst, src)
+            else:
+                nc.vector.tensor_copy(dst, src)
+            codes = sb("y_codes%d" % k, [P, width], U32)
+            nc.vector.quantize_mx(out=codes[:].bitcast(E4M3X4), scales=y_scales[:, starts[k] : starts[k] + width], in_=woven[:])
+            nc.sync.dma_start(out=words_out[:, starts[k] : starts[k] + width], in_=codes[:].bitcast(I32))
+        scales_out = out_2[0].bitcast(I32)
+        for q in range(4):
+            queue = nc.scalar if q % 2 == 0 else nc.sync
+            queue.dma_start(out=scales_out[4 * q : 4 * q + 4, :], in_=y_scales[32 * q : 32 * q + 4, :].bitcast(I32))

@@ -23,8 +23,9 @@ LANES = 4
 BLOCKS = SLOTS // P
 HALF = SLOTS // 2
 LIST_ROWS = 16
-CHUNKS = (256, 512, 512, 512, 256)
-SCALAR_WEAVES = (4,)
+CHUNKS = (256, 512, 512, 256, 256, 256)
+SCALAR_WEAVES = (4, 5)
+W_SPLIT = 80
 
 FLOPS = 2 * SLOTS * E * D
 
@@ -52,7 +53,7 @@ def tile_attend_gnorm_ln_pl_kernel(tc, xT, W, dz, gam, offs, out_0, out_1, out_2
         offsets = keep.tile([P, SLOTS // LIST_ROWS], U16, name="offsets")
         nc.sync.dma_start(offsets[:], offs)
         gam_col = sb("gam_col", [P, LANES], F32)
-        nc.scalar.dma_start(out=gam_col[:], in_=gam[0:1, :].rearrange("o (p t) -> (o p) t", t=LANES))
+        nc.sync.dma_start(out=gam_col[:], in_=gam[0:1, :].rearrange("o (p t) -> (o p) t", t=LANES))
         x_planes = xT.rearrange("(p t) c -> t p c", t=LANES)
         x_win = []
         for t in range(LANES):
@@ -63,10 +64,10 @@ def tile_attend_gnorm_ln_pl_kernel(tc, xT, W, dz, gam, offs, out_0, out_1, out_2
         ident = sb("ident", [P, P], F32)
         nc.vector.memset(ident[:], 0.0)
         make_identity(nc, ident[:], nomemset=True)
-        moments = sb("moments", [P, BLOCKS, LANES + 1, 3], F32)
-        nc.vector.memset(moments[:], float(P))
-        warm = sb("warm", [P, 1], F32)
-        nc.scalar.activation(warm[:], moments[:, 0, 0, 0:1], ACT.Sqrt)
+        moments = sb("moments", [P, BLOCKS, 5, 3], F32)
+        count_squared = sb("count_squared", [P, BLOCKS, 3], F32)
+        nc.vector.memset(count_squared[:], float(P * P))
+        nc.scalar.activation(moments[:, :, 0:3, 0], count_squared[:], ACT.Sqrt)
 
         y_win = []
         for t in range(LANES):
@@ -83,12 +84,14 @@ def tile_attend_gnorm_ln_pl_kernel(tc, xT, W, dz, gam, offs, out_0, out_1, out_2
         w_bf = sb("w_bf", [P, D * LANES], BF16)
         w_dst = w_bf[:].rearrange("p (t m j) -> p m t j", t=LANES, j=LANES)
         w_src = w_raw[:].rearrange("p j (m t) -> p m t j", t=LANES)
-        nc.scalar.copy(w_dst, w_src)
+        nc.vector.tensor_copy(w_dst[:, :W_SPLIT], w_src[:, :W_SPLIT])
+        nc.scalar.copy(w_dst[:, W_SPLIT:], w_src[:, W_SPLIT:])
         w_codes = sb("w_codes", [P, D], U32)
         w_scales = sb("w_scales", [P, D], U8)
         dz_bf = [sb("dz_bf%d" % a, [P, HALF, LANES], BF16) for a in range(2)]
-        for a in range(2):
-            nc.vector.tensor_copy(dz_bf[a][:], dz_raw[a][:].rearrange("p j i -> p i j"))
+        nc.vector.quantize_mx(out=w_codes[:].bitcast(E4M3X4), scales=w_scales[:], in_=w_bf[:])
+        nc.vector.tensor_copy(dz_bf[0][:], dz_raw[0][:].rearrange("p j i -> p i j"))
+        nc.scalar.copy(dz_bf[1][:], dz_raw[1][:].rearrange("p j i -> p i j"))
 
         dn = []
         for a in range(2):
@@ -96,8 +99,6 @@ def tile_attend_gnorm_ln_pl_kernel(tc, xT, W, dz, gam, offs, out_0, out_1, out_2
             scales = sb("dz_scales%d" % a, [P, HALF], U8)
             nc.vector.quantize_mx(
                 out=codes[:].bitcast(E5M2X4), scales=scales[:], in_=dz_bf[a][:].rearrange("p i j -> p (i j)"))
-            if a == 0:
-                nc.vector.quantize_mx(out=w_codes[:].bitcast(E4M3X4), scales=w_scales[:], in_=w_bf[:])
             for b in range(2):
                 acc = psum.tile([P, D], F32, name="dn%d" % (2 * a + b), tag="wide", bufs=4)
                 nc.tensor.matmul_mx(
@@ -117,16 +118,16 @@ def tile_attend_gnorm_ln_pl_kernel(tc, xT, W, dz, gam, offs, out_0, out_1, out_2
         turned = [psum.tile([P, D], F32, name="turned%d" % j, tag="x_bank%d" % j) for j in range(BLOCKS)]
         for t in range(LANES):
             plane = slice(t * P, (t + 1) * P)
+            if t < 2:
+                for j in (2 * t, 2 * t + 1):
+                    nc.vector.scalar_tensor_tensor(
+                        h[j][:], dn[j][:], 1.0, gam_row[:], ALU.mult, ALU.mult, accum_out=h1[:, j : j + 1])
             gathered = sb("xg%d" % t, [P, SLOTS], F32)
             parts = [(0, SLOTS)] if t < LANES - 1 else [(0, HALF), (HALF, HALF)]
             for first, count in parts:
                 nc.vector.tensor_copy(gathered[:, first : first + count], x_win[t][:].indirect(list_part(first, count)))
             for j in range(BLOCKS):
                 nc.tensor.transpose(turned[j][:, plane], gathered[:, j * P : (j + 1) * P], ident[:])
-            if t < 2:
-                for j in (2 * t, 2 * t + 1):
-                    nc.vector.scalar_tensor_tensor(
-                        h[j][:], dn[j][:], 1.0, gam_row[:], ALU.mult, ALU.mult, accum_out=h1[:, j : j + 1])
             if t < LANES - 1:
                 for a in range(2):
                     for j in (2 * a, 2 * a + 1):
@@ -136,12 +137,14 @@ def tile_attend_gnorm_ln_pl_kernel(tc, xT, W, dz, gam, offs, out_0, out_1, out_2
                         nc.scalar.activation(
                             unused[:, j, :], turned[j][:, plane], ACT.Square,
                             scale=-1.0, bias=moments[:, j, t, 1:2], accum_out=moments[:, j, t, 2:3])
+        products = [sb("products%d" % j, [P, D], F32) for j in range(BLOCKS)]
         h_mean = sb("h_mean", [P, BLOCKS], F32)
-        neg_h_mean = sb("neg_h_mean", [P, BLOCKS], F32)
-        nc.vector.tensor_scalar(h_mean[:], h1[:], 1.0 / D, None, ALU.mult)
-        nc.vector.tensor_scalar(neg_h_mean[:], h1[:], -1.0 / D, None, ALU.mult)
+        neg_h_late = sb("neg_h_late", [P, 2], F32)
+        neg_h_mean = [products[2][:, 0:1], products[3][:, 0:1], neg_h_late[:, 0:1], neg_h_late[:, 1:2]]
+        nc.scalar.activation(h_mean[:], h1[:], ACT.Copy, scale=1.0 / D)
+        for j in range(BLOCKS):
+            nc.scalar.activation(neg_h_mean[j], h1[:, j : j + 1], ACT.Copy, scale=-1.0 / D)
 
-        products = sb("products", [P, BLOCKS, D], F32)
         xh = sb("xh", [P, BLOCKS], F32)
         mv = sb("mv", [P, BLOCKS, 2], F32)
         inv_var = sb("inv_var", [P, BLOCKS], F32)
@@ -149,10 +152,11 @@ def tile_attend_gnorm_ln_pl_kernel(tc, xT, W, dz, gam, offs, out_0, out_1, out_2
         part = sb("part", [P, BLOCKS], F32)
         neg_mean = sb("neg_mean", [P, BLOCKS], F32)
         slope = sb("slope", [P, BLOCKS], F32)
-        shift = sb("shift", [P, BLOCKS], F32)
+        shift_early = sb("shift_early", [P, BLOCKS - 1], F32)
         rstd_row = sb("rstd_row", [P, SLOTS], F32)
         last = LANES - 1
-        u = []
+        u = [sb("u%d" % j, [P, D], F32) for j in range(BLOCKS)]
+        shift = [shift_early[:, j : j + 1] for j in range(BLOCKS - 1)] + [u[1][:, 0:1]]
         backs = [sb("back%d" % t, [P, SLOTS], F32) for t in range(LANES)]
 
         def turn_back(t, first, count, acc):
@@ -166,34 +170,32 @@ def tile_attend_gnorm_ln_pl_kernel(tc, xT, W, dz, gam, offs, out_0, out_1, out_2
             pair = slice(2 * a, 2 * a + 2)
             both = (2 * a, 2 * a + 1)
             for j in both:
-                nc.vector.bn_stats(moments[:, j, last:, :].rearrange("p t s -> p (t s)"), turned[j][:, last * P :])
+                nc.vector.bn_stats(moments[:, j, 3:5, :].rearrange("p t s -> p (t s)"), turned[j][:, last * P :])
             for j in both:
                 nc.vector.bn_aggr(mv[:, j, :], moments[:, j].rearrange("p t s -> p (t s)"))
+            nc.vector.reciprocal(inv_var[:, pair], mv[:, pair, 1])
+            nc.vector.tensor_tensor(part[:, pair], mv[:, pair, 0], h_mean[:, pair], ALU.mult)
+            nc.vector.tensor_scalar(neg_mean[:, pair], mv[:, pair, 0], -1.0, None, ALU.mult)
             for j in both:
                 col = slice(j, j + 1)
                 nc.vector.scalar_tensor_tensor(
-                    products[:, j, :], turned[j][:], 1.0 / D, h[j][:], ALU.mult, ALU.mult, accum_out=xh[:, col])
+                    products[j][:], turned[j][:], 1.0 / D, h[j][:], ALU.mult, ALU.mult, accum_out=xh[:, col])
                 if j == both[0]:
-                    nc.vector.reciprocal(inv_var[:, pair], mv[:, pair, 1])
-                    nc.vector.tensor_scalar(neg_mean[:, pair], mv[:, pair, 0], -1.0, None, ALU.mult)
-                    nc.vector.tensor_tensor(part[:, pair], mv[:, pair, 0], h_mean[:, pair], ALU.mult)
+                    nc.scalar.activation(rstd[:, pair], inv_var[:, pair], ACT.Sqrt)
+                    row_ps = psum.tile([P, HALF], F32, name="row_ps", tag="wide", bufs=4)
+                    for b in range(2):
+                        nc.tensor.transpose(
+                            row_ps[:, b * P : (b + 1) * P], rstd[:, j + b : j + b + 1].to_broadcast([P, P]), ident[:])
+                    nc.scalar.copy(rstd_row[:, a * HALF : (a + 1) * HALF], row_ps[:])
                 nc.vector.tensor_scalar(slope[:, col], part[:, col], xh[:, col], inv_var[:, col], ALU.subtract, ALU.mult)
-                nc.scalar.activation(shift[:, col], slope[:, col], ACT.Identity, scale=neg_mean[:, col], bias=neg_h_mean[:, col])
-                uj = sb("u%d" % j, [P, D], F32)
-                nc.scalar.activation(uj[:], turned[j][:], ACT.Identity, scale=slope[:, col], bias=shift[:, col])
-                u.append(uj)
-            nc.scalar.activation(rstd[:, pair], inv_var[:, pair], ACT.Sqrt)
-            row_ps = psum.tile([P, HALF], F32, name="row_ps", tag="wide", bufs=4)
-            for b in range(2):
-                j = 2 * a + b
-                nc.tensor.transpose(row_ps[:, b * P : (b + 1) * P], rstd[:, j : j + 1].to_broadcast([P, P]), ident[:])
-            nc.scalar.copy(rstd_row[:, a * HALF : (a + 1) * HALF], row_ps[:])
+                nc.vector.tensor_scalar(shift[j], slope[:, col], neg_mean[:, col], neg_h_mean[j], ALU.mult, ALU.add)
+                nc.scalar.activation(u[j][:], turned[j][:], ACT.Identity, scale=slope[:, col], bias=shift[j])
             turn_back(0, a * HALF, HALF, psum.tile([P, HALF], F32, name="back_half", tag="wide", bufs=4))
         for t in range(1, LANES):
             turn_back(t, 0, SLOTS, psum.tile([P, SLOTS], F32, name="back_whole", tag="x_bank%d" % (t - 1)))
 
         starts = [sum(CHUNKS[:k]) for k in range(len(CHUNKS))]
-        former = ("u3", "h_block3", "u2", "h_block2", "u1")
+        former = ("u3", "h_block3", "u2", "h_block2", "u1", "h_block1")
         y_planes = out_0.rearrange("(p t) c -> t p c", t=LANES)
         pairs = [sb("pairs%d" % k, [P, 2, width, 2], BF16, tag=former[k]) for k, width in enumerate(CHUNKS)]
         for t in range(LANES):

@@ -23,15 +23,17 @@ LANES = 4
 BLOCKS = SLOTS // P
 HALF = SLOTS // 2
 LIST_ROWS = 16
-CHUNKS = (256, 512, 512, 256, 256, 256)
-SCALAR_WEAVES = (4, 5)
+QUADRANT = 32
 W_SPLIT = 80
+CHUNKS = (256, 512, 512, 256, 256, 256)
+SCALAR_WEAVES = 2
 
 FLOPS = 2 * SLOTS * E * D
 
 
 def tile_attend_gnorm_ln_pl_kernel(tc, xT, W, dz, gam, offs, out_0, out_1, out_2):
     nc = tc.nc
+    last = LANES - 1
     with ExitStack() as ctx:
         keep = ctx.enter_context(tc.tile_pool(name="keep", bufs=1))
         psum = ctx.enter_context(tc.psum_pool(name="psum", bufs=1))
@@ -44,16 +46,12 @@ def tile_attend_gnorm_ln_pl_kernel(tc, xT, W, dz, gam, offs, out_0, out_1, out_2
 
         w_raw = sb("w_raw", [P, LANES, D], F32)
         nc.sync.dma_start(out=w_raw[:], in_=W.rearrange("(p j) d -> p j d", j=LANES))
-        dz_rows = dz.rearrange("(p j) i -> p j i", j=LANES)
-        dz_raw = []
-        for a in range(2):
-            raw = sb("dz_raw%d" % a, [P, LANES, HALF], F32)
-            nc.sync.dma_start(out=raw[:], in_=dz_rows[:, :, a * HALF : (a + 1) * HALF])
-            dz_raw.append(raw)
+        dz_raw = sb("dz_raw", [P, LANES, SLOTS], F32)
+        nc.sync.dma_start(out=dz_raw[:], in_=dz.rearrange("(p j) i -> p j i", j=LANES))
         offsets = keep.tile([P, SLOTS // LIST_ROWS], U16, name="offsets")
         nc.sync.dma_start(offsets[:], offs)
         gam_col = sb("gam_col", [P, LANES], F32)
-        nc.sync.dma_start(out=gam_col[:], in_=gam[0:1, :].rearrange("o (p t) -> (o p) t", t=LANES))
+        nc.scalar.dma_start(out=gam_col[:], in_=gam[0:1, :].rearrange("o (p t) -> (o p) t", t=LANES))
         x_planes = xT.rearrange("(p t) c -> t p c", t=LANES)
         x_win = []
         for t in range(LANES):
@@ -64,10 +62,11 @@ def tile_attend_gnorm_ln_pl_kernel(tc, xT, W, dz, gam, offs, out_0, out_1, out_2
         ident = sb("ident", [P, P], F32)
         nc.vector.memset(ident[:], 0.0)
         make_identity(nc, ident[:], nomemset=True)
-        moments = sb("moments", [P, BLOCKS, 5, 3], F32)
-        count_squared = sb("count_squared", [P, BLOCKS, 3], F32)
+
+        moments = sb("moments", [P, BLOCKS, LANES + 1, 3], F32)
+        count_squared = sb("count_squared", [P, BLOCKS, LANES], F32)
         nc.vector.memset(count_squared[:], float(P * P))
-        nc.scalar.activation(moments[:, :, 0:3, 0], count_squared[:], ACT.Sqrt)
+        nc.scalar.activation(moments[:, :, 0:LANES, 0], count_squared[:], ACT.Sqrt)
 
         y_win = []
         for t in range(LANES):
@@ -88,33 +87,34 @@ def tile_attend_gnorm_ln_pl_kernel(tc, xT, W, dz, gam, offs, out_0, out_1, out_2
         nc.scalar.copy(w_dst[:, W_SPLIT:], w_src[:, W_SPLIT:])
         w_codes = sb("w_codes", [P, D], U32)
         w_scales = sb("w_scales", [P, D], U8)
-        dz_bf = [sb("dz_bf%d" % a, [P, HALF, LANES], BF16) for a in range(2)]
         nc.vector.quantize_mx(out=w_codes[:].bitcast(E4M3X4), scales=w_scales[:], in_=w_bf[:])
-        nc.vector.tensor_copy(dz_bf[0][:], dz_raw[0][:].rearrange("p j i -> p i j"))
-        nc.scalar.copy(dz_bf[1][:], dz_raw[1][:].rearrange("p j i -> p i j"))
 
+        dz_bf = [sb("dz_bf%d" % a, [P, HALF, LANES], BF16) for a in range(2)]
+        dz_src = dz_raw[:].rearrange("p j i -> p i j")
+        nc.vector.tensor_copy(dz_bf[0][:], dz_src[:, :HALF])
+        nc.scalar.copy(dz_bf[1][:], dz_src[:, HALF:])
         dn = []
         for a in range(2):
-            codes = sb("dz_codes%d" % a, [P, HALF], U32)
-            scales = sb("dz_scales%d" % a, [P, HALF], U8)
+            dz_codes = sb("dz_codes%d" % a, [P, HALF], U32)
+            dz_scales = sb("dz_scales%d" % a, [P, HALF], U8)
             nc.vector.quantize_mx(
-                out=codes[:].bitcast(E5M2X4), scales=scales[:], in_=dz_bf[a][:].rearrange("p i j -> p (i j)"))
+                out=dz_codes[:].bitcast(E5M2X4), scales=dz_scales[:], in_=dz_bf[a][:].rearrange("p i j -> p (i j)"))
             for b in range(2):
-                acc = psum.tile([P, D], F32, name="dn%d" % (2 * a + b), tag="wide", bufs=4)
+                product = psum.tile([P, D], F32, name="dn%d" % (2 * a + b), tag="wide", bufs=BLOCKS)
                 nc.tensor.matmul_mx(
-                    out=acc[:],
-                    lhsT=codes[:, b * P : (b + 1) * P].bitcast(E5M2X4),
-                    lhsT_scale=scales[:, b * P : (b + 1) * P],
+                    out=product[:],
+                    lhsT=dz_codes[:, b * P : (b + 1) * P].bitcast(E5M2X4),
+                    lhsT_scale=dz_scales[:, b * P : (b + 1) * P],
                     rhs=w_codes[:].bitcast(E4M3X4),
                     rhs_scale=w_scales[:],
                     start=True,
                     stop=True,
                 )
-                dn.append(acc)
+                dn.append(product)
 
         h1 = sb("h1", [P, BLOCKS], F32)
         h = [sb("h_block%d" % j, [P, D], F32) for j in range(BLOCKS)]
-        unused = sb("unused", [P, BLOCKS, P], F32)
+        summands = sb("summands", [P, BLOCKS, P], F32)
         turned = [psum.tile([P, D], F32, name="turned%d" % j, tag="x_bank%d" % j) for j in range(BLOCKS)]
         for t in range(LANES):
             plane = slice(t * P, (t + 1) * P)
@@ -122,88 +122,88 @@ def tile_attend_gnorm_ln_pl_kernel(tc, xT, W, dz, gam, offs, out_0, out_1, out_2
                 for j in (2 * t, 2 * t + 1):
                     nc.vector.scalar_tensor_tensor(
                         h[j][:], dn[j][:], 1.0, gam_row[:], ALU.mult, ALU.mult, accum_out=h1[:, j : j + 1])
-            gathered = sb("xg%d" % t, [P, SLOTS], F32)
-            parts = [(0, SLOTS)] if t < LANES - 1 else [(0, HALF), (HALF, HALF)]
-            for first, count in parts:
+            gathered = sb("gathered%d" % t, [P, SLOTS], F32)
+            for first, count in [(0, SLOTS)] if t < last else [(0, HALF), (HALF, HALF)]:
                 nc.vector.tensor_copy(gathered[:, first : first + count], x_win[t][:].indirect(list_part(first, count)))
             for j in range(BLOCKS):
                 nc.tensor.transpose(turned[j][:, plane], gathered[:, j * P : (j + 1) * P], ident[:])
-            if t < LANES - 1:
-                for a in range(2):
-                    for j in (2 * a, 2 * a + 1):
-                        nc.scalar.activation(
-                            unused[:, j, :], turned[j][:, plane], ACT.Copy, scale=1.0 / P, accum_out=moments[:, j, t, 1:2])
-                    for j in (2 * a, 2 * a + 1):
-                        nc.scalar.activation(
-                            unused[:, j, :], turned[j][:, plane], ACT.Square,
-                            scale=-1.0, bias=moments[:, j, t, 1:2], accum_out=moments[:, j, t, 2:3])
-        products = [sb("products%d" % j, [P, D], F32) for j in range(BLOCKS)]
+            for a in range(2) if t < last else (1,):
+                for j in (2 * a, 2 * a + 1):
+                    nc.scalar.activation(
+                        summands[:, j, :], turned[j][:, plane], ACT.Copy, scale=1.0 / P, accum_out=moments[:, j, t, 1:2])
+                for j in (2 * a, 2 * a + 1):
+                    nc.scalar.activation(
+                        summands[:, j, :], turned[j][:, plane], ACT.Square,
+                        scale=-1.0, bias=moments[:, j, t, 1:2], accum_out=moments[:, j, t, 2:3])
+
+        xh_terms = [sb("xh_terms%d" % j, [P, D], F32) for j in range(BLOCKS)]
         h_mean = sb("h_mean", [P, BLOCKS], F32)
         neg_h_late = sb("neg_h_late", [P, 2], F32)
-        neg_h_mean = [products[2][:, 0:1], products[3][:, 0:1], neg_h_late[:, 0:1], neg_h_late[:, 1:2]]
+        neg_h_mean = [xh_terms[2][:, 0:1], xh_terms[3][:, 0:1], neg_h_late[:, 0:1], neg_h_late[:, 1:2]]
         nc.scalar.activation(h_mean[:], h1[:], ACT.Copy, scale=1.0 / D)
         for j in range(BLOCKS):
             nc.scalar.activation(neg_h_mean[j], h1[:, j : j + 1], ACT.Copy, scale=-1.0 / D)
 
         xh = sb("xh", [P, BLOCKS], F32)
-        mv = sb("mv", [P, BLOCKS, 2], F32)
+        mean_var = sb("mean_var", [P, BLOCKS, 2], F32)
         inv_var = sb("inv_var", [P, BLOCKS], F32)
         rstd = sb("rstd", [P, BLOCKS], F32)
-        part = sb("part", [P, BLOCKS], F32)
+        mean_h = sb("mean_h", [P, BLOCKS], F32)
         neg_mean = sb("neg_mean", [P, BLOCKS], F32)
         slope = sb("slope", [P, BLOCKS], F32)
-        shift_early = sb("shift_early", [P, BLOCKS - 1], F32)
+        shifts = sb("shifts", [P, BLOCKS - 1], F32)
         rstd_row = sb("rstd_row", [P, SLOTS], F32)
-        last = LANES - 1
         u = [sb("u%d" % j, [P, D], F32) for j in range(BLOCKS)]
-        shift = [shift_early[:, j : j + 1] for j in range(BLOCKS - 1)] + [u[1][:, 0:1]]
-        backs = [sb("back%d" % t, [P, SLOTS], F32) for t in range(LANES)]
+        shift = [shifts[:, 0:1], shifts[:, 1:2], u[1][:, 0:1], shifts[:, 2:3]]
+        unscaled = [sb("unscaled%d" % t, [P, SLOTS], F32) for t in range(LANES)]
 
-        def turn_back(t, first, count, acc):
+        def turn_back(t, first, count, bank):
             for j in range(first // P, (first + count) // P):
-                dst = acc[:, j * P - first : (j + 1) * P - first]
+                dst = bank[:, j * P - first : (j + 1) * P - first]
                 nc.tensor.matmul(dst, h[j][:, t * P : (t + 1) * P], ident[:], start=True, stop=False, is_transpose=True)
                 nc.tensor.matmul(dst, u[j][:, t * P : (t + 1) * P], ident[:], start=False, stop=True, is_transpose=True)
-            nc.scalar.copy(backs[t][:, first : first + count], acc[:])
+            nc.scalar.copy(unscaled[t][:, first : first + count], bank[:])
 
         for a in range(2):
             pair = slice(2 * a, 2 * a + 2)
             both = (2 * a, 2 * a + 1)
+            if a == 0:
+                for j in both:
+                    nc.vector.bn_stats(moments[:, j, last:, :].rearrange("p t s -> p (t s)"), turned[j][:, last * P :])
+            triples = LANES + 1 if a == 0 else LANES
             for j in both:
-                nc.vector.bn_stats(moments[:, j, 3:5, :].rearrange("p t s -> p (t s)"), turned[j][:, last * P :])
+                nc.vector.bn_aggr(mean_var[:, j, :], moments[:, j, :triples].rearrange("p t s -> p (t s)"))
+            nc.vector.reciprocal(inv_var[:, pair], mean_var[:, pair, 1])
             for j in both:
-                nc.vector.bn_aggr(mv[:, j, :], moments[:, j].rearrange("p t s -> p (t s)"))
-            nc.vector.reciprocal(inv_var[:, pair], mv[:, pair, 1])
-            nc.vector.tensor_tensor(part[:, pair], mv[:, pair, 0], h_mean[:, pair], ALU.mult)
-            nc.vector.tensor_scalar(neg_mean[:, pair], mv[:, pair, 0], -1.0, None, ALU.mult)
+                nc.scalar.activation(mean_h[:, j : j + 1], mean_var[:, j, 0:1], ACT.Copy, scale=h_mean[:, j : j + 1])
+            nc.scalar.activation(neg_mean[:, pair], mean_var[:, pair, 0], ACT.Copy, scale=-1.0)
+            nc.scalar.activation(rstd[:, pair], inv_var[:, pair], ACT.Sqrt)
+            row_ps = psum.tile([P, HALF], F32, name="row_ps", tag="wide", bufs=BLOCKS)
+            for b, j in enumerate(both):
+                nc.tensor.transpose(row_ps[:, b * P : (b + 1) * P], rstd[:, j : j + 1].to_broadcast([P, P]), ident[:])
+            nc.scalar.copy(rstd_row[:, a * HALF : (a + 1) * HALF], row_ps[:])
             for j in both:
                 col = slice(j, j + 1)
                 nc.vector.scalar_tensor_tensor(
-                    products[j][:], turned[j][:], 1.0 / D, h[j][:], ALU.mult, ALU.mult, accum_out=xh[:, col])
-                if j == both[0]:
-                    nc.scalar.activation(rstd[:, pair], inv_var[:, pair], ACT.Sqrt)
-                    row_ps = psum.tile([P, HALF], F32, name="row_ps", tag="wide", bufs=4)
-                    for b in range(2):
-                        nc.tensor.transpose(
-                            row_ps[:, b * P : (b + 1) * P], rstd[:, j + b : j + b + 1].to_broadcast([P, P]), ident[:])
-                    nc.scalar.copy(rstd_row[:, a * HALF : (a + 1) * HALF], row_ps[:])
-                nc.vector.tensor_scalar(slope[:, col], part[:, col], xh[:, col], inv_var[:, col], ALU.subtract, ALU.mult)
+                    xh_terms[j][:], turned[j][:], 1.0 / D, h[j][:], ALU.mult, ALU.mult, accum_out=xh[:, col])
+                nc.vector.tensor_scalar(slope[:, col], mean_h[:, col], xh[:, col], inv_var[:, col], ALU.subtract, ALU.mult)
                 nc.vector.tensor_scalar(shift[j], slope[:, col], neg_mean[:, col], neg_h_mean[j], ALU.mult, ALU.add)
-                nc.scalar.activation(u[j][:], turned[j][:], ACT.Identity, scale=slope[:, col], bias=shift[j])
-            turn_back(0, a * HALF, HALF, psum.tile([P, HALF], F32, name="back_half", tag="wide", bufs=4))
+                if j == BLOCKS - 1:
+                    nc.vector.tensor_scalar(u[j][:], turned[j][:], slope[:, col], shift[j], ALU.mult, ALU.add)
+                else:
+                    nc.scalar.activation(u[j][:], turned[j][:], ACT.Identity, scale=slope[:, col], bias=shift[j])
+            turn_back(0, a * HALF, HALF, psum.tile([P, HALF], F32, name="back_half", tag="wide", bufs=BLOCKS))
         for t in range(1, LANES):
             turn_back(t, 0, SLOTS, psum.tile([P, SLOTS], F32, name="back_whole", tag="x_bank%d" % (t - 1)))
 
         starts = [sum(CHUNKS[:k]) for k in range(len(CHUNKS))]
-        former = ("u3", "h_block3", "u2", "h_block2", "u1", "h_block1")
+        freed = ("u3", "h_block3", "u2", "h_block2", "u1", "h_block1")
         y_planes = out_0.rearrange("(p t) c -> t p c", t=LANES)
-        pairs = [sb("pairs%d" % k, [P, 2, width, 2], BF16, tag=former[k]) for k, width in enumerate(CHUNKS)]
+        pairs = [sb("pairs%d" % k, [P, 2, width, 2], BF16, tag=freed[k]) for k, width in enumerate(CHUNKS)]
         for t in range(LANES):
-            back = backs[t]
-            parts = [(0, HALF), (HALF, HALF)] if t == 0 else [(0, SLOTS)]
-            for first, count in parts:
+            for first, count in [(0, HALF), (HALF, HALF)] if t == 0 else [(0, SLOTS)]:
                 nc.vector.tensor_tensor(
-                    y_win[t][:].indirect(list_part(first, count)), back[:, first : first + count],
+                    y_win[t][:].indirect(list_part(first, count)), unscaled[t][:, first : first + count],
                     rstd_row[:, first : first + count], ALU.mult)
             nc.sync.dma_start(out=y_planes[t], in_=y_win[t][:])
             for k, width in enumerate(CHUNKS):
@@ -212,17 +212,20 @@ def tile_attend_gnorm_ln_pl_kernel(tc, xT, W, dz, gam, offs, out_0, out_1, out_2
         words_out = out_1[0].rearrange("p c l -> p (c l)").bitcast(I32)
         y_scales = sb("y_scales", [P, TOKENS], U8)
         for k, width in enumerate(CHUNKS):
+            cols = slice(starts[k], starts[k] + width)
             woven = sb("woven%d" % k, [P, width * LANES], BF16)
             src = pairs[k][:].rearrange("p a c b -> p (a c b)").bitcast(F32).rearrange("p (a c) -> p c a", a=2)
             dst = woven[:].bitcast(F32).rearrange("p (c a) -> p c a", a=2)
-            if k in SCALAR_WEAVES:
+            if k >= len(CHUNKS) - SCALAR_WEAVES:
                 nc.scalar.copy(dst, src)
             else:
                 nc.vector.tensor_copy(dst, src)
-            codes = sb("y_codes%d" % k, [P, width], U32)
-            nc.vector.quantize_mx(out=codes[:].bitcast(E4M3X4), scales=y_scales[:, starts[k] : starts[k] + width], in_=woven[:])
-            nc.sync.dma_start(out=words_out[:, starts[k] : starts[k] + width], in_=codes[:].bitcast(I32))
+            y_codes = sb("y_codes%d" % k, [P, width], U32)
+            nc.vector.quantize_mx(out=y_codes[:].bitcast(E4M3X4), scales=y_scales[:, cols], in_=woven[:])
+            nc.sync.dma_start(out=words_out[:, cols], in_=y_codes[:].bitcast(I32))
         scales_out = out_2[0].bitcast(I32)
-        for q in range(4):
+        for q in range(P // QUADRANT):
             queue = nc.scalar if q % 2 == 0 else nc.sync
-            queue.dma_start(out=scales_out[4 * q : 4 * q + 4, :], in_=y_scales[32 * q : 32 * q + 4, :].bitcast(I32))
+            queue.dma_start(
+                out=scales_out[LANES * q : LANES * (q + 1), :],
+                in_=y_scales[QUADRANT * q : QUADRANT * q + LANES, :].bitcast(I32))

from contextlib import ExitStack

import concourse.mybir as mybir
from concourse.masks import make_identity

F32 = mybir.dt.float32
BF16 = mybir.dt.bfloat16
I32 = mybir.dt.int32
U32 = mybir.dt.uint32
U16 = mybir.dt.uint16
U8 = mybir.dt.uint8
E4M3X4 = mybir.dt.float8_e4m3fn_x4
E5M2X4 = mybir.dt.float8_e5m2_x4
ALU = mybir.AluOpType
ACT = mybir.ActivationFunctionType

P = 128
D = 512
E = 512
SLOTS = 512
TOKENS = 2048
LANES = 4
BLOCKS = SLOTS // P
HALF = SLOTS // 2
LIST_ROWS = 16
QUADRANT = 32
W_SPLIT = 80
CHUNKS = (256, 512, 512, 256, 256, 256)
SCALAR_WEAVES = 2

FLOPS = 2 * SLOTS * E * D


def tile_attend_gnorm_ln_pl_kernel(tc, xT, W, dz, gam, offs, out_0, out_1, out_2):
    nc = tc.nc
    last = LANES - 1
    with ExitStack() as ctx:
        keep = ctx.enter_context(tc.tile_pool(name="keep", bufs=1))
        psum = ctx.enter_context(tc.psum_pool(name="psum", bufs=1))

        def sb(name, shape, dtype, tag=""):
            return keep.tile(shape, dtype, name=name, tag=tag or name, align_bytes=64)

        def list_part(first, count):
            return offsets[:, first // LIST_ROWS : (first + count) // LIST_ROWS]

        w_raw = sb("w_raw", [P, LANES, D], F32)
        nc.sync.dma_start(out=w_raw[:], in_=W.rearrange("(p j) d -> p j d", j=LANES))
        dz_raw = sb("dz_raw", [P, LANES, SLOTS], F32)
        nc.sync.dma_start(out=dz_raw[:], in_=dz.rearrange("(p j) i -> p j i", j=LANES))
        offsets = keep.tile([P, SLOTS // LIST_ROWS], U16, name="offsets")
        nc.sync.dma_start(offsets[:], offs)
        gam_col = sb("gam_col", [P, LANES], F32)
        nc.scalar.dma_start(out=gam_col[:], in_=gam[0:1, :].rearrange("o (p t) -> (o p) t", t=LANES))
        x_planes = xT.rearrange("(p t) c -> t p c", t=LANES)
        x_win = []
        for t in range(LANES):
            win = sb("x_win%d" % t, [P, TOKENS], F32)
            nc.sync.dma_start(out=win[:], in_=x_planes[t])
            x_win.append(win)

        ident = sb("ident", [P, P], F32)
        nc.vector.memset(ident[:], 0.0)
        make_identity(nc, ident[:], nomemset=True)

        moments = sb("moments", [P, BLOCKS, LANES + 1, 3], F32)
        count_squared = sb("count_squared", [P, BLOCKS, LANES], F32)
        nc.vector.memset(count_squared[:], float(P * P))
        nc.scalar.activation(moments[:, :, 0:LANES, 0], count_squared[:], ACT.Sqrt)

        y_win = []
        for t in range(LANES):
            win = sb("y_win%d" % t, [P, TOKENS], F32)
            nc.vector.memset(win[:].bitcast(I32), 0)
            y_win.append(win)

        gam_ps = psum.tile([P, LANES, P], F32, name="gam_ps", tag="x_bank3")
        for t in range(LANES):
            nc.tensor.transpose(gam_ps[:, t, :], gam_col[:, t : t + 1].to_broadcast([P, P]), ident[:])
        gam_row = sb("gam_row", [P, D], F32)
        nc.scalar.copy(gam_row[:], gam_ps[:].rearrange("q t p -> q (t p)"))

        w_bf = sb("w_bf", [P, D * LANES], BF16)
        w_dst = w_bf[:].rearrange("p (t m j) -> p m t j", t=LANES, j=LANES)
        w_src = w_raw[:].rearrange("p j (m t) -> p m t j", t=LANES)
        nc.vector.tensor_copy(w_dst[:, :W_SPLIT], w_src[:, :W_SPLIT])
        nc.scalar.copy(w_dst[:, W_SPLIT:], w_src[:, W_SPLIT:])
        w_codes = sb("w_codes", [P, D], U32)
        w_scales = sb("w_scales", [P, D], U8)
        nc.vector.quantize_mx(out=w_codes[:].bitcast(E4M3X4), scales=w_scales[:], in_=w_bf[:])

        dz_bf = [sb("dz_bf%d" % a, [P, HALF, LANES], BF16) for a in range(2)]
        dz_src = dz_raw[:].rearrange("p j i -> p i j")
        nc.vector.tensor_copy(dz_bf[0][:], dz_src[:, :HALF])
        nc.scalar.copy(dz_bf[1][:], dz_src[:, HALF:])
        dn = []
        for a in range(2):
            dz_codes = sb("dz_codes%d" % a, [P, HALF], U32)
            dz_scales = sb("dz_scales%d" % a, [P, HALF], U8)
            nc.vector.quantize_mx(
                out=dz_codes[:].bitcast(E5M2X4), scales=dz_scales[:], in_=dz_bf[a][:].rearrange("p i j -> p (i j)"))
            for b in range(2):
                product = psum.tile([P, D], F32, name="dn%d" % (2 * a + b), tag="wide", bufs=BLOCKS)
                nc.tensor.matmul_mx(
                    out=product[:],
                    lhsT=dz_codes[:, b * P : (b + 1) * P].bitcast(E5M2X4),
                    lhsT_scale=dz_scales[:, b * P : (b + 1) * P],
                    rhs=w_codes[:].bitcast(E4M3X4),
                    rhs_scale=w_scales[:],
                    start=True,
                    stop=True,
                )
                dn.append(product)

        h1 = sb("h1", [P, BLOCKS], F32)
        h = [sb("h_block%d" % j, [P, D], F32) for j in range(BLOCKS)]
        summands = sb("summands", [P, BLOCKS, P], F32)
        turned = [psum.tile([P, D], F32, name="turned%d" % j, tag="x_bank%d" % j) for j in range(BLOCKS)]
        for t in range(LANES):
            plane = slice(t * P, (t + 1) * P)
            if t < 2:
                for j in (2 * t, 2 * t + 1):
                    nc.vector.scalar_tensor_tensor(
                        h[j][:], dn[j][:], 1.0, gam_row[:], ALU.mult, ALU.mult, accum_out=h1[:, j : j + 1])
            gathered = sb("gathered%d" % t, [P, SLOTS], F32)
            for first, count in [(0, SLOTS)] if t < last else [(0, HALF), (HALF, HALF)]:
                nc.vector.tensor_copy(gathered[:, first : first + count], x_win[t][:].indirect(list_part(first, count)))
            for j in range(BLOCKS):
                nc.tensor.transpose(turned[j][:, plane], gathered[:, j * P : (j + 1) * P], ident[:])
            for a in range(2) if t < last else (1,):
                for j in (2 * a, 2 * a + 1):
                    nc.scalar.activation(
                        summands[:, j, :], turned[j][:, plane], ACT.Copy, scale=1.0 / P, accum_out=moments[:, j, t, 1:2])
                for j in (2 * a, 2 * a + 1):
                    nc.scalar.activation(
                        summands[:, j, :], turned[j][:, plane], ACT.Square,
                        scale=-1.0, bias=moments[:, j, t, 1:2], accum_out=moments[:, j, t, 2:3])

        xh_terms = [sb("xh_terms%d" % j, [P, D], F32) for j in range(BLOCKS)]
        h_mean = sb("h_mean", [P, BLOCKS], F32)
        neg_h_late = sb("neg_h_late", [P, 2], F32)
        neg_h_mean = [xh_terms[2][:, 0:1], xh_terms[3][:, 0:1], neg_h_late[:, 0:1], neg_h_late[:, 1:2]]
        nc.scalar.activation(h_mean[:], h1[:], ACT.Copy, scale=1.0 / D)
        for j in range(BLOCKS):
            nc.scalar.activation(neg_h_mean[j], h1[:, j : j + 1], ACT.Copy, scale=-1.0 / D)

        xh = sb("xh", [P, BLOCKS], F32)
        mean_var = sb("mean_var", [P, BLOCKS, 2], F32)
        inv_var = sb("inv_var", [P, BLOCKS], F32)
        rstd = sb("rstd", [P, BLOCKS], F32)
        mean_h = sb("mean_h", [P, BLOCKS], F32)
        neg_mean = sb("neg_mean", [P, BLOCKS], F32)
        slope = sb("slope", [P, BLOCKS], F32)
        shifts = sb("shifts", [P, BLOCKS - 1], F32)
        rstd_row = sb("rstd_row", [P, SLOTS], F32)
        u = [sb("u%d" % j, [P, D], F32) for j in range(BLOCKS)]
        shift = [shifts[:, 0:1], shifts[:, 1:2], u[1][:, 0:1], shifts[:, 2:3]]
        unscaled = [sb("unscaled%d" % t, [P, SLOTS], F32) for t in range(LANES)]

        def turn_back(t, first, count, bank):
            for j in range(first // P, (first + count) // P):
                dst = bank[:, j * P - first : (j + 1) * P - first]
                nc.tensor.matmul(dst, h[j][:, t * P : (t + 1) * P], ident[:], start=True, stop=False, is_transpose=True)
                nc.tensor.matmul(dst, u[j][:, t * P : (t + 1) * P], ident[:], start=False, stop=True, is_transpose=True)
            nc.scalar.copy(unscaled[t][:, first : first + count], bank[:])

        for a in range(2):
            pair = slice(2 * a, 2 * a + 2)
            both = (2 * a, 2 * a + 1)
            if a == 0:
                for j in both:
                    nc.vector.bn_stats(moments[:, j, last:, :].rearrange("p t s -> p (t s)"), turned[j][:, last * P :])
            triples = LANES + 1 if a == 0 else LANES
            for j in both:
                nc.vector.bn_aggr(mean_var[:, j, :], moments[:, j, :triples].rearrange("p t s -> p (t s)"))
            nc.vector.reciprocal(inv_var[:, pair], mean_var[:, pair, 1])
            for j in both:
                nc.scalar.activation(mean_h[:, j : j + 1], mean_var[:, j, 0:1], ACT.Copy, scale=h_mean[:, j : j + 1])
            nc.scalar.activation(neg_mean[:, pair], mean_var[:, pair, 0], ACT.Copy, scale=-1.0)
            nc.scalar.activation(rstd[:, pair], inv_var[:, pair], ACT.Sqrt)
            row_ps = psum.tile([P, HALF], F32, name="row_ps", tag="wide", bufs=BLOCKS)
            for b, j in enumerate(both):
                nc.tensor.transpose(row_ps[:, b * P : (b + 1) * P], rstd[:, j : j + 1].to_broadcast([P, P]), ident[:])
            nc.scalar.copy(rstd_row[:, a * HALF : (a + 1) * HALF], row_ps[:])
            for j in both:
                col = slice(j, j + 1)
                nc.vector.scalar_tensor_tensor(
                    xh_terms[j][:], turned[j][:], 1.0 / D, h[j][:], ALU.mult, ALU.mult, accum_out=xh[:, col])
                nc.vector.tensor_scalar(slope[:, col], mean_h[:, col], xh[:, col], inv_var[:, col], ALU.subtract, ALU.mult)
                nc.vector.tensor_scalar(shift[j], slope[:, col], neg_mean[:, col], neg_h_mean[j], ALU.mult, ALU.add)
                if j == BLOCKS - 1:
                    nc.vector.tensor_scalar(u[j][:], turned[j][:], slope[:, col], shift[j], ALU.mult, ALU.add)
                else:
                    nc.scalar.activation(u[j][:], turned[j][:], ACT.Identity, scale=slope[:, col], bias=shift[j])
            turn_back(0, a * HALF, HALF, psum.tile([P, HALF], F32, name="back_half", tag="wide", bufs=BLOCKS))
        for t in range(1, LANES):
            turn_back(t, 0, SLOTS, psum.tile([P, SLOTS], F32, name="back_whole", tag="x_bank%d" % (t - 1)))

        starts = [sum(CHUNKS[:k]) for k in range(len(CHUNKS))]
        freed = ("u3", "h_block3", "u2", "h_block2", "u1", "h_block1")
        y_planes = out_0.rearrange("(p t) c -> t p c", t=LANES)
        pairs = [sb("pairs%d" % k, [P, 2, width, 2], BF16, tag=freed[k]) for k, width in enumerate(CHUNKS)]
        for t in range(LANES):
            for first, count in [(0, HALF), (HALF, HALF)] if t == 0 else [(0, SLOTS)]:
                nc.vector.tensor_tensor(
                    y_win[t][:].indirect(list_part(first, count)), unscaled[t][:, first : first + count],
                    rstd_row[:, first : first + count], ALU.mult)
            nc.sync.dma_start(out=y_planes[t], in_=y_win[t][:])
            for k, width in enumerate(CHUNKS):
                nc.scalar.copy(pairs[k][:, t // 2, :, t % 2], y_win[t][:, starts[k] : starts[k] + width])

        words_out = out_1[0].rearrange("p c l -> p (c l)").bitcast(I32)
        y_scales = sb("y_scales", [P, TOKENS], U8)
        for k, width in enumerate(CHUNKS):
            cols = slice(starts[k], starts[k] + width)
            woven = sb("woven%d" % k, [P, width * LANES], BF16)
            src = pairs[k][:].rearrange("p a c b -> p (a c b)").bitcast(F32).rearrange("p (a c) -> p c a", a=2)
            dst = woven[:].bitcast(F32).rearrange("p (c a) -> p c a", a=2)
            if k >= len(CHUNKS) - SCALAR_WEAVES:
                nc.scalar.copy(dst, src)
            else:
                nc.vector.tensor_copy(dst, src)
            y_codes = sb("y_codes%d" % k, [P, width], U32)
            nc.vector.quantize_mx(out=y_codes[:].bitcast(E4M3X4), scales=y_scales[:, cols], in_=woven[:])
            nc.sync.dma_start(out=words_out[:, cols], in_=y_codes[:].bitcast(I32))
        scales_out = out_2[0].bitcast(I32)
        for q in range(P // QUADRANT):
            queue = nc.scalar if q % 2 == 0 else nc.sync
            queue.dma_start(
                out=scales_out[LANES * q : LANES * (q + 1), :],
                in_=y_scales[QUADRANT * q : QUADRANT * q + LANES, :].bitcast(I32))
